import numpy as np
import ml_dtypes


def mxq(x, axis, fmt="e4m3"):
    dtype, down = {"e4m3": (ml_dtypes.float8_e4m3fn, 7), "e5m2": (ml_dtypes.float8_e5m2, 14)}[fmt]
    v = np.moveaxis(np.asarray(x, np.float32).astype(ml_dtypes.bfloat16).astype(np.float64), axis, -1)
    blocks = v.reshape(v.shape[:-1] + (-1, 32))
    amax = np.abs(blocks).max(-1, keepdims=True)
    byte = np.maximum(np.where(amax > 0, np.frexp(amax)[1] - 1 + 127, 0) - down, 1)
    scale = np.exp2(byte - 127.0)
    codes = (blocks / scale).astype(np.float32).astype(dtype).astype(np.float64)
    return np.moveaxis((codes * scale).reshape(v.shape), -1, axis)


WIDE = False


def mx_kscale(k):
    if not WIDE:
        return np.ones(k)
    levels = np.array([30, -30])
    if k % 512:
        return np.exp2(np.random.permutation(np.resize(levels, k // 32))).repeat(32)
    a = np.empty((k // 512, 16))
    for p in range(k // 512):
        a[p, :8] = np.random.permutation(np.resize(levels, 8))
        for g in range(8):
            far = levels[np.abs(levels - a[p, g]) >= 10]
            a[p, g + 8] = far[np.random.randint(len(far))]
    return np.exp2(a.ravel()).repeat(32)


def f64(x):
    return np.asarray(x).astype(np.float64)


def striped(idx):
    return np.tile(np.asarray(idx).reshape(-1, 16).T, (8, 1)).astype(np.uint16)


def unstriped(offs):
    return offs[:16].T.reshape(-1).astype(np.int64)


E2M1 = np.array([0.0, 0.5, 1.0, 1.5, 2.0, 3.0, 4.0, 6.0, -0.0, -0.5, -1.0, -1.5, -2.0, -3.0, -4.0, -6.0])


def pack_weight(w, fmt):
    k, n = w.shape
    w = f64(np.asarray(w, np.float32).astype(ml_dtypes.bfloat16)).reshape(k // 32, 32, n)
    amax = np.abs(w).max(1)
    if fmt in ("e4m3", "e5m2"):
        byte = np.frexp(amax)[1] - 1 + 127 - (7 if fmt == "e4m3" else 14)
    else:
        mant, ex = np.frexp(amax / 6.0)
        byte = np.where(mant > 0.5, ex, ex - 1) + 127
    byte = np.clip(np.where(amax > 0, byte, 1), 1, 254)
    scaled = (w * np.exp2(127.0 - byte)[:, None, :]).reshape(k, n).astype(np.float32)
    by_word = np.ascontiguousarray(scaled.reshape(k // 512, 128, 4, n).transpose(0, 1, 3, 2))
    if fmt in ("e4m3", "e5m2"):
        words = by_word.astype(ml_dtypes.float8_e4m3fn if fmt == "e4m3" else ml_dtypes.float8_e5m2).view(np.uint8)
    else:
        c = by_word.astype(ml_dtypes.float4_e2m1fn).view(np.uint8) & 0xF
        words = (c[..., 0::2] | (c[..., 1::2] << 4)).reshape(k // 512, 128, 2 * n)
    return np.ascontiguousarray(words), np.ascontiguousarray(byte.astype(np.uint8).reshape(k // 512, 16, n))


def unpack_weight(words, scales, fmt):
    g, _, n = scales.shape
    words = np.ascontiguousarray(words).reshape(g, 128, n, -1)
    if fmt in ("e4m3", "e5m2"):
        vals = words.view(ml_dtypes.float8_e4m3fn if fmt == "e4m3" else ml_dtypes.float8_e5m2).astype(np.float64)
    else:
        nib = np.empty((g, 128, n, 4), np.uint8)
        nib[..., 0::2] = words & 0xF
        nib[..., 1::2] = words >> 4
        vals = E2M1[nib]
    vals = vals * np.repeat(np.exp2(scales.astype(np.float64) - 127.0), 8, axis=1)[..., None]
    return vals.transpose(0, 1, 3, 2).reshape(g * 512, n)


K, T, J, R, V, N, E = 512, 1024, 256, 512, 512, 256, 1024


def setup_inputs():
    n = np.random.standard_normal
    idx = np.random.permutation(T)[:J]
    idx2 = np.random.permutation(V)[:J]
    idx3 = np.random.permutation(V)[:J]
    idx4 = np.random.permutation(T)[:J]
    idx5 = np.random.permutation(E)[:J]
    fk = mx_kscale(K)
    fr = mx_kscale(R)
    xtp = pack_weight(n((K, T)) / fk[:, None], "e4m3")
    wp = pack_weight(n((K, R)) * 1 / np.sqrt(K) * fk[:, None] * fr, "e2m1")
    wbp = pack_weight(n((R, N)) * 1 / np.sqrt(R) / fr[:, None], "e5m2")
    wsp = pack_weight(n((K, N)) * 1 / np.sqrt(K) * fk[:, None], "e5m2")
    return {
        "xt_words": xtp[0],
        "xt_scales": xtp[1],
        "w_words": wp[0],
        "w_scales": wp[1],
        "tb": (n((R, V)) * 0.8 * fr[:, None]).astype(np.float32),
        "wb_words": wbp[0],
        "wb_scales": wbp[1],
        "ws_words": wsp[0],
        "ws_scales": wsp[1],
        "offs": striped(idx),
        "offs2": striped(idx2),
        "offs3": striped(idx3),
        "offs4": striped(idx4),
        "offs5": striped(idx5),
    }


def reference(xt_words, xt_scales, w_words, w_scales, tb, wb_words, wb_scales, ws_words, ws_scales, offs, offs2, offs3, offs4, offs5):
    idx = unstriped(offs)
    idx2 = unstriped(offs2)
    idx3 = unstriped(offs3)
    idx4 = unstriped(offs4)
    idx5 = unstriped(offs5)
    xtu = unpack_weight(xt_words, xt_scales, "e4m3")
    wu = unpack_weight(w_words, w_scales, "e2m1")
    wbu = unpack_weight(wb_words, wb_scales, "e5m2")
    wsu = unpack_weight(ws_words, ws_scales, "e5m2")
    xtidxg = xtu[:, idx]
    a = wu.T @ xtidxg
    hid = np.maximum(np.minimum(a, f64(tb)[:, idx2]), f64(tb)[:, idx3])
    hidq = mxq(hid, 0, "e4m3")
    xtidx4g = xtu[:, idx4]
    p = wbu.T @ hidq + wsu.T @ xtidx4g
    y = np.zeros((N, E))
    y[:, idx5] = p
    return y

@@ -1,0 +1,176 @@
+from contextlib import ExitStack
+
+import concourse.mybir as mybir
+
+K, T, J, R, V, N, E = 512, 1024, 256, 512, 512, 256, 1024
+FLOPS = 2 * J * (K * R + R * N + K * N)
+
+F32 = mybir.dt.float32
+BF16 = mybir.dt.bfloat16
+I32 = mybir.dt.int32
+U32 = mybir.dt.uint32
+U16 = mybir.dt.uint16
+U8 = mybir.dt.uint8
+E4M3 = mybir.dt.float8_e4m3fn_x4
+E5M2 = mybir.dt.float8_e5m2_x4
+E2M1 = mybir.dt.float4_e2m1fn_x4
+COPY = mybir.ActivationFunctionType.Copy
+MIN = mybir.AluOpType.min
+MAX = mybir.AluOpType.max
+
+P = 128
+PACK = 4
+QUADS = 4
+
+
+def load_scale_rows(queue, plane, rows):
+    for q in range(QUADS):
+        queue.dma_start(
+            out=plane[32 * q : 32 * q + 4, :].bitcast(I32),
+            in_=rows[0, 4 * q : 4 * q + 4, :].bitcast(I32),
+        )
+
+
+def words_of(packed):
+    return packed[0].rearrange("p c b -> p (c b)").bitcast(I32)
+
+
+def tile_list_clamped_solo_further_scattered_kernel(
+    tc, xt_words, xt_scales, w_words, w_scales, tb, wb_words, wb_scales, ws_words, ws_scales,
+    offs, offs2, offs3, offs4, offs5, out,
+):
+    nc = tc.nc
+    with ExitStack() as ctx:
+        lists = ctx.enter_context(tc.tile_pool(name="lists", bufs=1))
+        sb = ctx.enter_context(tc.tile_pool(name="sb", bufs=1))
+        psum = ctx.enter_context(tc.psum_pool(name="psum", bufs=1))
+
+        token_list = lists.tile([P, J // 16], U16, name="token_list")
+        upper_list = lists.tile([P, J // 16], U16, name="upper_list")
+        lower_list = lists.tile([P, J // 16], U16, name="lower_list")
+        short_list = lists.tile([P, J // 16], U16, name="short_list")
+        place_list = lists.tile([P, J // 16], U16, name="place_list")
+
+        x_codes = sb.tile([P, T], U32, name="x_codes", align_bytes=64)
+        x_plane = sb.tile([P, T], U8, name="x_plane", align_bytes=64)
+        w_raw = sb.tile([P, 2 * R], U8, name="w_raw", align_bytes=64)
+        w_codes = sb.tile([P, 2 * R], U8, name="w_codes", align_bytes=64)
+        w_plane = sb.tile([P, R], U8, name="w_plane", align_bytes=64)
+        wb_codes = sb.tile([P, N], U32, name="wb_codes", align_bytes=64)
+        ws_codes = sb.tile([P, N], U32, name="ws_codes", align_bytes=64)
+        w_raw_plane = sb.tile([P, R], U8, name="w_raw_plane", align_bytes=64)
+        wb_plane = sb.tile([P, N], U8, name="wb_plane", align_bytes=64)
+        ws_plane = sb.tile([P, N], U8, name="ws_plane", align_bytes=64)
+        bounds = [sb.tile([P, 2 * V], F32, name=f"bounds{a}", align_bytes=64) for a in range(2)]
+        pages = [sb.tile([P, E], F32, name=f"page{n}", align_bytes=64) for n in range(2)]
+
+        nc.vector.memset(x_plane[:].bitcast(I32), 0)
+        nc.gpsimd.memset(ws_plane[:].bitcast(I32), 0)
+        nc.vector.memset(w_raw_plane[:].bitcast(I32), 0)
+        nc.vector.memset(wb_plane[:].bitcast(I32), 0)
+        nc.vector.memset(pages[0][:], 0.0)
+        nc.vector.memset(pages[1][:], 0.0)
+
+        tb_rows = tb.rearrange("(p t) v -> p (t v)", t=PACK)
+        load_scale_rows(nc.gpsimd, ws_plane, ws_scales)
+        nc.sync.dma_start(upper_list[:], offs2)
+        nc.sync.dma_start(out=bounds[0][:], in_=tb_rows[:, 0 : 2 * V])
+        nc.sync.dma_start(token_list[:], offs)
+        load_scale_rows(nc.sync, x_plane, xt_scales)
+        nc.sync.dma_start(out=x_codes[:].bitcast(I32), in_=words_of(xt_words))
+        nc.sync.dma_start(lower_list[:], offs3)
+        nc.sync.dma_start(out=w_raw[:].bitcast(I32), in_=w_words[0].bitcast(I32))
+        nc.sync.dma_start(out=bounds[1][:], in_=tb_rows[:, 2 * V : 4 * V])
+        load_scale_rows(nc.sync, w_raw_plane, w_scales)
+        nc.sync.dma_start(short_list[:], offs4)
+        nc.sync.dma_start(out=ws_codes[:].bitcast(I32), in_=words_of(ws_words))
+        nc.sync.dma_start(out=wb_codes[:].bitcast(I32), in_=words_of(wb_words))
+        load_scale_rows(nc.sync, wb_plane, wb_scales)
+        nc.sync.dma_start(place_list[:], offs5)
+
+        upper = sb.tile([P, PACK, J], F32, name="upper", align_bytes=64)
+        lower = sb.tile([P, PACK, J], F32, name="lower", align_bytes=64)
+        for a in range(2):
+            for picked, entries in ((upper, upper_list), (lower, lower_list)):
+                for t in (2 * a, 2 * a + 1):
+                    window = bounds[a][:, (t % 2) * V : (t % 2 + 1) * V]
+                    nc.scalar.activation(picked[:, t, :], window.indirect(entries[:]), COPY)
+
+        tok_codes = sb.tile([P, J], U32, name="tok_codes", align_bytes=64)
+        tok_plane = sb.tile([P, J], U8, name="tok_plane", align_bytes=64)
+        short_codes = sb.tile([P, J], U32, name="short_codes", align_bytes=64)
+        short_plane = sb.tile([P, J], U8, name="short_plane", align_bytes=64)
+        nc.vector.tensor_copy(tok_codes[:], x_codes[:].indirect(token_list[:]))
+        nc.vector.tensor_copy(tok_plane[:], x_plane[:].indirect(token_list[:]))
+        nc.vector.tensor_copy(
+            out=w_codes[:].bitcast(U16).rearrange("p (t m) -> p t m", t=PACK),
+            in_=w_raw[:].bitcast(U16).rearrange("p (m t) -> p t m", t=PACK),
+        )
+
+        nc.vector.tensor_copy(
+            out=w_plane[:].rearrange("p (t m) -> p t m", t=PACK),
+            in_=w_raw_plane[:].rearrange("p (m t) -> p t m", t=PACK),
+        )
+        nc.vector.tensor_copy(short_codes[:], x_codes[:].indirect(short_list[:]))
+        nc.vector.tensor_copy(short_plane[:], x_plane[:].indirect(short_list[:]))
+
+        a_banks = [psum.tile([P, 2, J], F32, name=f"a_bank{a}") for a in range(2)]
+        for t in range(PACK):
+            nc.tensor.matmul_mx(
+                out=a_banks[t // 2][:, t % 2, :],
+                lhsT=w_codes[:, 2 * P * t : 2 * P * (t + 1)].bitcast(E2M1),
+                lhsT_scale=w_plane[:, P * t : P * (t + 1)],
+                rhs=tok_codes[:].bitcast(E4M3),
+                rhs_scale=tok_plane[:],
+                start=True,
+                stop=True,
+            )
+        p_banks = [psum.tile([P, J], F32, name=f"p_bank{n}") for n in range(2)]
+        for n in range(2):
+            nc.tensor.matmul_mx(
+                out=p_banks[n][:],
+                lhsT=ws_codes[:, P * n : P * (n + 1)].bitcast(E5M2),
+                lhsT_scale=ws_plane[:, P * n : P * (n + 1)],
+                rhs=short_codes[:].bitcast(E4M3),
+                rhs_scale=short_plane[:],
+                start=True,
+                stop=False,
+            )
+
+        capped = sb.tile([P, PACK, J], F32, name="capped", align_bytes=64)
+        for a in range(2):
+            nc.vector.tensor_tensor(
+                out=capped[:, 2 * a : 2 * a + 2, :],
+                in0=a_banks[a][:],
+                in1=upper[:, 2 * a : 2 * a + 2, :],
+                op=MIN,
+            )
+        hid = sb.tile([P, PACK * J], BF16, name="hid", align_bytes=64)
+        nc.vector.tensor_tensor(
+            out=hid[:].rearrange("p (c i t) -> p c t i", i=4, t=PACK),
+            in0=capped[:].rearrange("p t (c i) -> p c t i", i=4),
+            in1=lower[:].rearrange("p t (c i) -> p c t i", i=4),
+            op=MAX,
+        )
+        hid_codes = sb.tile([P, J], U32, name="hid_codes", align_bytes=64)
+        hid_plane = sb.tile([P, J], U8, name="hid_plane", align_bytes=64)
+        nc.vector.quantize_mx(out=hid_codes[:].bitcast(E4M3), scales=hid_plane[:], in_=hid[:])
+
+        for n in range(2):
+            nc.tensor.matmul_mx(
+                out=p_banks[n][:],
+                lhsT=wb_codes[:, P * n : P * (n + 1)].bitcast(E5M2),
+                lhsT_scale=wb_plane[:, P * n : P * (n + 1)],
+                rhs=hid_codes[:].bitcast(E4M3),
+                rhs_scale=hid_plane[:],
+                start=False,
+                stop=True,
+            )
+
+        results = [sb.tile([P, J], F32, name=f"result{n}", align_bytes=64) for n in range(2)]
+        nc.vector.tensor_copy(results[0][:], p_banks[0][:])
+        nc.vector.tensor_copy(pages[0][:].indirect(place_list[:]), results[0][:])
+        nc.sync.dma_start(out=out[0:P, :], in_=pages[0][:])
+        nc.scalar.copy(results[1][:], p_banks[1][:])
+        nc.scalar.activation(pages[1][:].indirect(place_list[:]), results[1][:], COPY)
+        nc.scalar.dma_start(out=out[P : 2 * P, :], in_=pages[1][:])

@@ -23,8 +23,8 @@ PACK = 4
 QUADS = 4
 
 
-def load_scale_rows(queue, plane, rows):
-    for q in range(QUADS):
+def load_scale_rows(queue, plane, rows, quadrants=range(QUADS)):
+    for q in quadrants:
         queue.dma_start(
             out=plane[32 * q : 32 * q + 4, :].bitcast(I32),
             in_=rows[0, 4 * q : 4 * q + 4, :].bitcast(I32),
@@ -64,24 +64,28 @@ def tile_list_clamped_solo_further_scattered_kernel(
         bounds = [sb.tile([P, 2 * V], F32, name=f"bounds{a}", align_bytes=64) for a in range(2)]
         pages = [sb.tile([P, E], F32, name=f"page{n}", align_bytes=64) for n in range(2)]
 
-        nc.vector.memset(x_plane[:].bitcast(I32), 0)
+        tb_rows = tb.rearrange("(p t) v -> p (t v)", t=PACK)
+        warm_in = sb.tile([P, 1], F32, name="warm_in")
+        warm_out = sb.tile([P, 1], F32, name="warm_out")
+        nc.gpsimd.memset(w_raw_plane[:].bitcast(I32), 0)
+        nc.gpsimd.memset(x_plane[:].bitcast(I32), 0)
+        load_scale_rows(nc.gpsimd, x_plane, xt_scales, range(3, 4))
         nc.gpsimd.memset(ws_plane[:].bitcast(I32), 0)
-        nc.vector.memset(w_raw_plane[:].bitcast(I32), 0)
+        load_scale_rows(nc.gpsimd, ws_plane, ws_scales)
+        nc.vector.memset(warm_in[:], 0.0)
+        nc.scalar.activation(warm_out[:], warm_in[:], COPY)
         nc.vector.memset(wb_plane[:].bitcast(I32), 0)
         nc.vector.memset(pages[0][:], 0.0)
         nc.vector.memset(pages[1][:], 0.0)
-
-        tb_rows = tb.rearrange("(p t) v -> p (t v)", t=PACK)
-        load_scale_rows(nc.gpsimd, ws_plane, ws_scales)
         nc.sync.dma_start(upper_list[:], offs2)
-        nc.sync.dma_start(out=bounds[0][:], in_=tb_rows[:, 0 : 2 * V])
-        nc.sync.dma_start(token_list[:], offs)
-        load_scale_rows(nc.sync, x_plane, xt_scales)
-        nc.sync.dma_start(out=x_codes[:].bitcast(I32), in_=words_of(xt_words))
-        nc.sync.dma_start(lower_list[:], offs3)
         nc.sync.dma_start(out=w_raw[:].bitcast(I32), in_=w_words[0].bitcast(I32))
-        nc.sync.dma_start(out=bounds[1][:], in_=tb_rows[:, 2 * V : 4 * V])
         load_scale_rows(nc.sync, w_raw_plane, w_scales)
+        nc.sync.dma_start(out=bounds[0][:], in_=tb_rows[:, 0 : 2 * V])
+        nc.sync.dma_start(out=x_codes[:].bitcast(I32), in_=words_of(xt_words))
+        nc.sync.dma_start(token_list[:], offs)
+        nc.sync.dma_start(lower_list[:], offs3)
+        load_scale_rows(nc.sync, x_plane, xt_scales, range(0, 3))
+        nc.sync.dma_start(out=bounds[1][:], in_=tb_rows[:, 2 * V : 4 * V])
         nc.sync.dma_start(short_list[:], offs4)
         nc.sync.dma_start(out=ws_codes[:].bitcast(I32), in_=words_of(ws_words))
         nc.sync.dma_start(out=wb_codes[:].bitcast(I32), in_=words_of(wb_words))
@@ -90,87 +94,112 @@ def tile_list_clamped_solo_further_scattered_kernel(
 
         upper = sb.tile([P, PACK, J], F32, name="upper", align_bytes=64)
         lower = sb.tile([P, PACK, J], F32, name="lower", align_bytes=64)
-        for a in range(2):
-            for picked, entries in ((upper, upper_list), (lower, lower_list)):
-                for t in (2 * a, 2 * a + 1):
-                    window = bounds[a][:, (t % 2) * V : (t % 2 + 1) * V]
-                    nc.scalar.activation(picked[:, t, :], window.indirect(entries[:]), COPY)
+
+        def picked_bounds(t, entries):
+            return bounds[t // 2][:, (t % 2) * V : (t % 2 + 1) * V].indirect(entries[:])
+
+        nc.scalar.activation(upper[:, 0, :], picked_bounds(0, upper_list), COPY)
+        nc.scalar.activation(lower[:, 0, :], picked_bounds(0, lower_list), COPY)
+        nc.scalar.activation(lower[:, 1, :], picked_bounds(1, lower_list), COPY)
+        nc.scalar.activation(upper[:, 2, :], picked_bounds(2, upper_list), COPY)
+        nc.scalar.activation(upper[:, 3, :], picked_bounds(3, upper_list), COPY)
+        nc.scalar.activation(lower[:, 2, :], picked_bounds(2, lower_list), COPY)
+        nc.scalar.activation(lower[:, 3, :], picked_bounds(3, lower_list), COPY)
 
         tok_codes = sb.tile([P, J], U32, name="tok_codes", align_bytes=64)
         tok_plane = sb.tile([P, J], U8, name="tok_plane", align_bytes=64)
         short_codes = sb.tile([P, J], U32, name="short_codes", align_bytes=64)
         short_plane = sb.tile([P, J], U8, name="short_plane", align_bytes=64)
-        nc.vector.tensor_copy(tok_codes[:], x_codes[:].indirect(token_list[:]))
-        nc.vector.tensor_copy(tok_plane[:], x_plane[:].indirect(token_list[:]))
         nc.vector.tensor_copy(
             out=w_codes[:].bitcast(U16).rearrange("p (t m) -> p t m", t=PACK),
             in_=w_raw[:].bitcast(U16).rearrange("p (m t) -> p t m", t=PACK),
         )
-
         nc.vector.tensor_copy(
             out=w_plane[:].rearrange("p (t m) -> p t m", t=PACK),
             in_=w_raw_plane[:].rearrange("p (m t) -> p t m", t=PACK),
         )
+        nc.vector.tensor_copy(upper[:, 1, :], picked_bounds(1, upper_list))
+        nc.vector.tensor_copy(tok_codes[:], x_codes[:].indirect(token_list[:]))
+        nc.vector.tensor_copy(tok_plane[:], x_plane[:].indirect(token_list[:]))
         nc.vector.tensor_copy(short_codes[:], x_codes[:].indirect(short_list[:]))
         nc.vector.tensor_copy(short_plane[:], x_plane[:].indirect(short_list[:]))
 
-        a_banks = [psum.tile([P, 2, J], F32, name=f"a_bank{a}") for a in range(2)]
-        for t in range(PACK):
-            nc.tensor.matmul_mx(
-                out=a_banks[t // 2][:, t % 2, :],
-                lhsT=w_codes[:, 2 * P * t : 2 * P * (t + 1)].bitcast(E2M1),
-                lhsT_scale=w_plane[:, P * t : P * (t + 1)],
-                rhs=tok_codes[:].bitcast(E4M3),
-                rhs_scale=tok_plane[:],
-                start=True,
-                stop=True,
-            )
-        p_banks = [psum.tile([P, J], F32, name=f"p_bank{n}") for n in range(2)]
-        for n in range(2):
-            nc.tensor.matmul_mx(
-                out=p_banks[n][:],
-                lhsT=ws_codes[:, P * n : P * (n + 1)].bitcast(E5M2),
-                lhsT_scale=ws_plane[:, P * n : P * (n + 1)],
-                rhs=short_codes[:].bitcast(E4M3),
-                rhs_scale=short_plane[:],
-                start=True,
-                stop=False,
-            )
+        H = J // 2
+        halves = [slice(0, H), slice(H, J)]
+        a_banks = [psum.tile([P, PACK, H], F32, name=f"a_bank{h}") for h in range(2)]
+        for h in range(2):
+            for t in range(PACK):
+                nc.tensor.matmul_mx(
+                    out=a_banks[h][:, t, :],
+                    lhsT=w_codes[:, 2 * P * t : 2 * P * (t + 1)].bitcast(E2M1),
+                    lhsT_scale=w_plane[:, P * t : P * (t + 1)],
+                    rhs=tok_codes[:, halves[h]].bitcast(E4M3),
+                    rhs_scale=tok_plane[:, halves[h]],
+                    start=True,
+                    stop=True,
+                )
+        p_banks = [[psum.tile([P, H], F32, name=f"p_bank{h}{n}") for n in range(2)] for h in range(2)]
+        for h in range(2):
+            for n in range(2):
+                nc.tensor.matmul_mx(
+                    out=p_banks[h][n][:],
+                    lhsT=ws_codes[:, P * n : P * (n + 1)].bitcast(E5M2),
+                    lhsT_scale=ws_plane[:, P * n : P * (n + 1)],
+                    rhs=short_codes[:, halves[h]].bitcast(E4M3),
+                    rhs_scale=short_plane[:, halves[h]],
+                    start=True,
+                    stop=False,
+                )
 
-        capped = sb.tile([P, PACK, J], F32, name="capped", align_bytes=64)
-        for a in range(2):
+        capped = [sb.tile([P, PACK, H], F32, name=f"capped{h}", align_bytes=64) for h in range(2)]
+        hid = [sb.tile([P, PACK * H], BF16, name=f"hid{h}", align_bytes=64) for h in range(2)]
+        hid_codes = [sb.tile([P, H], U32, name=f"hid_codes{h}", align_bytes=64) for h in range(2)]
+        hid_plane = [sb.tile([P, H], U8, name=f"hid_plane{h}", align_bytes=64) for h in range(2)]
+        results = [[sb.tile([P, H], F32, name=f"result{h}{n}", align_bytes=64) for n in range(2)] for h in range(2)]
+
+        def cap(h):
+            nc.vector.tensor_tensor(out=capped[h][:], in0=a_banks[h][:], in1=upper[:, :, halves[h]], op=MIN)
+
+        def floor(h):
             nc.vector.tensor_tensor(
-                out=capped[:, 2 * a : 2 * a + 2, :],
-                in0=a_banks[a][:],
-                in1=upper[:, 2 * a : 2 * a + 2, :],
-                op=MIN,
-            )
-        hid = sb.tile([P, PACK * J], BF16, name="hid", align_bytes=64)
-        nc.vector.tensor_tensor(
-            out=hid[:].rearrange("p (c i t) -> p c t i", i=4, t=PACK),
-            in0=capped[:].rearrange("p t (c i) -> p c t i", i=4),
-            in1=lower[:].rearrange("p t (c i) -> p c t i", i=4),
-            op=MAX,
-        )
-        hid_codes = sb.tile([P, J], U32, name="hid_codes", align_bytes=64)
-        hid_plane = sb.tile([P, J], U8, name="hid_plane", align_bytes=64)
-        nc.vector.quantize_mx(out=hid_codes[:].bitcast(E4M3), scales=hid_plane[:], in_=hid[:])
-
-        for n in range(2):
-            nc.tensor.matmul_mx(
-                out=p_banks[n][:],
-                lhsT=wb_codes[:, P * n : P * (n + 1)].bitcast(E5M2),
-                lhsT_scale=wb_plane[:, P * n : P * (n + 1)],
-                rhs=hid_codes[:].bitcast(E4M3),
-                rhs_scale=hid_plane[:],
-                start=False,
-                stop=True,
+                out=hid[h][:].rearrange("p (c i t) -> p c t i", i=2, t=PACK),
+                in0=capped[h][:].rearrange("p t (c i) -> p c t i", i=2),
+                in1=lower[:, :, halves[h]].rearrange("p t (c i) -> p c t i", i=2),
+                op=MAX,
             )
 
-        results = [sb.tile([P, J], F32, name=f"result{n}", align_bytes=64) for n in range(2)]
-        nc.vector.tensor_copy(results[0][:], p_banks[0][:])
-        nc.vector.tensor_copy(pages[0][:].indirect(place_list[:]), results[0][:])
-        nc.sync.dma_start(out=out[0:P, :], in_=pages[0][:])
-        nc.scalar.copy(results[1][:], p_banks[1][:])
-        nc.scalar.activation(pages[1][:].indirect(place_list[:]), results[1][:], COPY)
-        nc.scalar.dma_start(out=out[P : 2 * P, :], in_=pages[1][:])
+        def quantise(h):
+            nc.vector.quantize_mx(out=hid_codes[h][:].bitcast(E4M3), scales=hid_plane[h][:], in_=hid[h][:])
+            for n in range(2):
+                nc.tensor.matmul_mx(
+                    out=p_banks[h][n][:],
+                    lhsT=wb_codes[:, P * n : P * (n + 1)].bitcast(E5M2),
+                    lhsT_scale=wb_plane[:, P * n : P * (n + 1)],
+                    rhs=hid_codes[h][:].bitcast(E4M3),
+                    rhs_scale=hid_plane[h][:],
+                    start=False,
+                    stop=True,
+                )
+
+        def places(n, h):
+            return pages[n][:].indirect(place_list[:, h * H // 16 : (h + 1) * H // 16])
+
+        def place_on_scalar(h, n):
+            nc.scalar.copy(results[h][n][:], p_banks[h][n][:])
+            nc.scalar.activation(places(n, h), results[h][n][:], COPY)
+
+        def place_on_vector(h, n):
+            nc.vector.tensor_copy(results[h][n][:], p_banks[h][n][:])
+            nc.vector.tensor_copy(places(n, h), results[h][n][:])
+
+        cap(0)
+        cap(1)
+        floor(0)
+        floor(1)
+        quantise(0)
+        quantise(1)
+        for h in range(2):
+            place_on_scalar(h, 0)
+            place_on_vector(h, 1)
+        nc.scalar.dma_start(out=out[0:P, :], in_=pages[0][:])
+        nc.sync.dma_start(out=out[P : 2 * P, :], in_=pages[1][:])

@@ -67,24 +67,24 @@ def tile_list_clamped_solo_further_scattered_kernel(
         tb_rows = tb.rearrange("(p t) v -> p (t v)", t=PACK)
         warm_in = sb.tile([P, 1], F32, name="warm_in")
         warm_out = sb.tile([P, 1], F32, name="warm_out")
-        nc.gpsimd.memset(w_raw_plane[:].bitcast(I32), 0)
         nc.gpsimd.memset(x_plane[:].bitcast(I32), 0)
         load_scale_rows(nc.gpsimd, x_plane, xt_scales, range(3, 4))
         nc.gpsimd.memset(ws_plane[:].bitcast(I32), 0)
         load_scale_rows(nc.gpsimd, ws_plane, ws_scales)
         nc.vector.memset(warm_in[:], 0.0)
         nc.scalar.activation(warm_out[:], warm_in[:], COPY)
+        nc.vector.memset(w_raw_plane[:].bitcast(I32), 0)
         nc.vector.memset(wb_plane[:].bitcast(I32), 0)
         nc.vector.memset(pages[0][:], 0.0)
         nc.vector.memset(pages[1][:], 0.0)
         nc.sync.dma_start(upper_list[:], offs2)
+        nc.sync.dma_start(lower_list[:], offs3)
         nc.sync.dma_start(out=w_raw[:].bitcast(I32), in_=w_words[0].bitcast(I32))
-        load_scale_rows(nc.sync, w_raw_plane, w_scales)
+        load_scale_rows(nc.sync, x_plane, xt_scales, range(0, 3))
         nc.sync.dma_start(out=bounds[0][:], in_=tb_rows[:, 0 : 2 * V])
         nc.sync.dma_start(out=x_codes[:].bitcast(I32), in_=words_of(xt_words))
         nc.sync.dma_start(token_list[:], offs)
-        nc.sync.dma_start(lower_list[:], offs3)
-        load_scale_rows(nc.sync, x_plane, xt_scales, range(0, 3))
+        load_scale_rows(nc.sync, w_raw_plane, w_scales)
         nc.sync.dma_start(out=bounds[1][:], in_=tb_rows[:, 2 * V : 4 * V])
         nc.sync.dma_start(short_list[:], offs4)
         nc.sync.dma_start(out=ws_codes[:].bitcast(I32), in_=words_of(ws_words))
@@ -114,13 +114,13 @@ def tile_list_clamped_solo_further_scattered_kernel(
             out=w_codes[:].bitcast(U16).rearrange("p (t m) -> p t m", t=PACK),
             in_=w_raw[:].bitcast(U16).rearrange("p (m t) -> p t m", t=PACK),
         )
+        nc.vector.tensor_copy(upper[:, 1, :], picked_bounds(1, upper_list))
+        nc.vector.tensor_copy(tok_codes[:], x_codes[:].indirect(token_list[:]))
+        nc.vector.tensor_copy(tok_plane[:], x_plane[:].indirect(token_list[:]))
         nc.vector.tensor_copy(
             out=w_plane[:].rearrange("p (t m) -> p t m", t=PACK),
             in_=w_raw_plane[:].rearrange("p (m t) -> p t m", t=PACK),
         )
-        nc.vector.tensor_copy(upper[:, 1, :], picked_bounds(1, upper_list))
-        nc.vector.tensor_copy(tok_codes[:], x_codes[:].indirect(token_list[:]))
-        nc.vector.tensor_copy(tok_plane[:], x_plane[:].indirect(token_list[:]))
         nc.vector.tensor_copy(short_codes[:], x_codes[:].indirect(short_list[:]))
         nc.vector.tensor_copy(short_plane[:], x_plane[:].indirect(short_list[:]))
 

from contextlib import ExitStack

import concourse.mybir as mybir

K, T, J, R, V, N, E = 512, 1024, 256, 512, 512, 256, 1024
FLOPS = 2 * J * (K * R + R * N + K * N)

F32 = mybir.dt.float32
BF16 = mybir.dt.bfloat16
I32 = mybir.dt.int32
U32 = mybir.dt.uint32
U16 = mybir.dt.uint16
U8 = mybir.dt.uint8
E4M3 = mybir.dt.float8_e4m3fn_x4
E5M2 = mybir.dt.float8_e5m2_x4
E2M1 = mybir.dt.float4_e2m1fn_x4
COPY = mybir.ActivationFunctionType.Copy
MIN = mybir.AluOpType.min
MAX = mybir.AluOpType.max

P = 128
PACK = 4
QUADS = 4


def load_scale_rows(queue, plane, rows, quadrants=range(QUADS)):
    for q in quadrants:
        queue.dma_start(
            out=plane[32 * q : 32 * q + 4, :].bitcast(I32),
            in_=rows[0, 4 * q : 4 * q + 4, :].bitcast(I32),
        )


def words_of(packed):
    return packed[0].rearrange("p c b -> p (c b)").bitcast(I32)


def tile_list_clamped_solo_further_scattered_kernel(
    tc, xt_words, xt_scales, w_words, w_scales, tb, wb_words, wb_scales, ws_words, ws_scales,
    offs, offs2, offs3, offs4, offs5, out,
):
    nc = tc.nc
    with ExitStack() as ctx:
        lists = ctx.enter_context(tc.tile_pool(name="lists", bufs=1))
        sb = ctx.enter_context(tc.tile_pool(name="sb", bufs=1))
        psum = ctx.enter_context(tc.psum_pool(name="psum", bufs=1))

        token_list = lists.tile([P, J // 16], U16, name="token_list")
        upper_list = lists.tile([P, J // 16], U16, name="upper_list")
        lower_list = lists.tile([P, J // 16], U16, name="lower_list")
        short_list = lists.tile([P, J // 16], U16, name="short_list")
        place_list = lists.tile([P, J // 16], U16, name="place_list")

        x_codes = sb.tile([P, T], U32, name="x_codes", align_bytes=64)
        x_plane = sb.tile([P, T], U8, name="x_plane", align_bytes=64)
        w_raw = sb.tile([P, 2 * R], U8, name="w_raw", align_bytes=64)
        w_codes = sb.tile([P, 2 * R], U8, name="w_codes", align_bytes=64)
        w_plane = sb.tile([P, R], U8, name="w_plane", align_bytes=64)
        wb_codes = sb.tile([P, N], U32, name="wb_codes", align_bytes=64)
        ws_codes = sb.tile([P, N], U32, name="ws_codes", align_bytes=64)
        w_raw_plane = sb.tile([P, R], U8, name="w_raw_plane", align_bytes=64)
        wb_plane = sb.tile([P, N], U8, name="wb_plane", align_bytes=64)
        ws_plane = sb.tile([P, N], U8, name="ws_plane", align_bytes=64)
        bounds = [sb.tile([P, 2 * V], F32, name=f"bounds{a}", align_bytes=64) for a in range(2)]
        pages = [sb.tile([P, E], F32, name=f"page{n}", align_bytes=64) for n in range(2)]

        tb_rows = tb.rearrange("(p t) v -> p (t v)", t=PACK)
        warm_in = sb.tile([P, 1], F32, name="warm_in")
        warm_out = sb.tile([P, 1], F32, name="warm_out")
        nc.gpsimd.memset(x_plane[:].bitcast(I32), 0)
        load_scale_rows(nc.gpsimd, x_plane, xt_scales, range(3, 4))
        nc.gpsimd.memset(ws_plane[:].bitcast(I32), 0)
        load_scale_rows(nc.gpsimd, ws_plane, ws_scales)
        nc.vector.memset(warm_in[:], 0.0)
        nc.scalar.activation(warm_out[:], warm_in[:], COPY)
        nc.vector.memset(w_raw_plane[:].bitcast(I32), 0)
        nc.vector.memset(wb_plane[:].bitcast(I32), 0)
        nc.vector.memset(pages[0][:], 0.0)
        nc.vector.memset(pages[1][:], 0.0)
        nc.sync.dma_start(upper_list[:], offs2)
        nc.sync.dma_start(lower_list[:], offs3)
        nc.sync.dma_start(out=w_raw[:].bitcast(I32), in_=w_words[0].bitcast(I32))
        load_scale_rows(nc.sync, x_plane, xt_scales, range(0, 3))
        nc.sync.dma_start(out=bounds[0][:], in_=tb_rows[:, 0 : 2 * V])
        nc.sync.dma_start(out=x_codes[:].bitcast(I32), in_=words_of(xt_words))
        nc.sync.dma_start(token_list[:], offs)
        load_scale_rows(nc.sync, w_raw_plane, w_scales)
        nc.sync.dma_start(out=bounds[1][:], in_=tb_rows[:, 2 * V : 4 * V])
        nc.sync.dma_start(short_list[:], offs4)
        nc.sync.dma_start(out=ws_codes[:].bitcast(I32), in_=words_of(ws_words))
        nc.sync.dma_start(out=wb_codes[:].bitcast(I32), in_=words_of(wb_words))
        load_scale_rows(nc.sync, wb_plane, wb_scales)
        nc.sync.dma_start(place_list[:], offs5)

        upper = sb.tile([P, PACK, J], F32, name="upper", align_bytes=64)
        lower = sb.tile([P, PACK, J], F32, name="lower", align_bytes=64)

        def picked_bounds(t, entries):
            return bounds[t // 2][:, (t % 2) * V : (t % 2 + 1) * V].indirect(entries[:])

        nc.scalar.activation(upper[:, 0, :], picked_bounds(0, upper_list), COPY)
        nc.scalar.activation(lower[:, 0, :], picked_bounds(0, lower_list), COPY)
        nc.scalar.activation(lower[:, 1, :], picked_bounds(1, lower_list), COPY)
        nc.scalar.activation(upper[:, 2, :], picked_bounds(2, upper_list), COPY)
        nc.scalar.activation(upper[:, 3, :], picked_bounds(3, upper_list), COPY)
        nc.scalar.activation(lower[:, 2, :], picked_bounds(2, lower_list), COPY)
        nc.scalar.activation(lower[:, 3, :], picked_bounds(3, lower_list), COPY)

        tok_codes = sb.tile([P, J], U32, name="tok_codes", align_bytes=64)
        tok_plane = sb.tile([P, J], U8, name="tok_plane", align_bytes=64)
        short_codes = sb.tile([P, J], U32, name="short_codes", align_bytes=64)
        short_plane = sb.tile([P, J], U8, name="short_plane", align_bytes=64)
        nc.vector.tensor_copy(
            out=w_codes[:].bitcast(U16).rearrange("p (t m) -> p t m", t=PACK),
            in_=w_raw[:].bitcast(U16).rearrange("p (m t) -> p t m", t=PACK),
        )
        nc.vector.tensor_copy(upper[:, 1, :], picked_bounds(1, upper_list))
        nc.vector.tensor_copy(tok_codes[:], x_codes[:].indirect(token_list[:]))
        nc.vector.tensor_copy(tok_plane[:], x_plane[:].indirect(token_list[:]))
        nc.vector.tensor_copy(
            out=w_plane[:].rearrange("p (t m) -> p t m", t=PACK),
            in_=w_raw_plane[:].rearrange("p (m t) -> p t m", t=PACK),
        )
        nc.vector.tensor_copy(short_codes[:], x_codes[:].indirect(short_list[:]))
        nc.vector.tensor_copy(short_plane[:], x_plane[:].indirect(short_list[:]))

        H = J // 2
        halves = [slice(0, H), slice(H, J)]
        a_banks = [psum.tile([P, PACK, H], F32, name=f"a_bank{h}") for h in range(2)]
        for h in range(2):
            for t in range(PACK):
                nc.tensor.matmul_mx(
                    out=a_banks[h][:, t, :],
                    lhsT=w_codes[:, 2 * P * t : 2 * P * (t + 1)].bitcast(E2M1),
                    lhsT_scale=w_plane[:, P * t : P * (t + 1)],
                    rhs=tok_codes[:, halves[h]].bitcast(E4M3),
                    rhs_scale=tok_plane[:, halves[h]],
                    start=True,
                    stop=True,
                )
        p_banks = [[psum.tile([P, H], F32, name=f"p_bank{h}{n}") for n in range(2)] for h in range(2)]
        for h in range(2):
            for n in range(2):
                nc.tensor.matmul_mx(
                    out=p_banks[h][n][:],
                    lhsT=ws_codes[:, P * n : P * (n + 1)].bitcast(E5M2),
                    lhsT_scale=ws_plane[:, P * n : P * (n + 1)],
                    rhs=short_codes[:, halves[h]].bitcast(E4M3),
                    rhs_scale=short_plane[:, halves[h]],
                    start=True,
                    stop=False,
                )

        capped = [sb.tile([P, PACK, H], F32, name=f"capped{h}", align_bytes=64) for h in range(2)]
        hid = [sb.tile([P, PACK * H], BF16, name=f"hid{h}", align_bytes=64) for h in range(2)]
        hid_codes = [sb.tile([P, H], U32, name=f"hid_codes{h}", align_bytes=64) for h in range(2)]
        hid_plane = [sb.tile([P, H], U8, name=f"hid_plane{h}", align_bytes=64) for h in range(2)]
        results = [[sb.tile([P, H], F32, name=f"result{h}{n}", align_bytes=64) for n in range(2)] for h in range(2)]

        def cap(h):
            nc.vector.tensor_tensor(out=capped[h][:], in0=a_banks[h][:], in1=upper[:, :, halves[h]], op=MIN)

        def floor(h):
            nc.vector.tensor_tensor(
                out=hid[h][:].rearrange("p (c i t) -> p c t i", i=2, t=PACK),
                in0=capped[h][:].rearrange("p t (c i) -> p c t i", i=2),
                in1=lower[:, :, halves[h]].rearrange("p t (c i) -> p c t i", i=2),
                op=MAX,
            )

        def quantise(h):
            nc.vector.quantize_mx(out=hid_codes[h][:].bitcast(E4M3), scales=hid_plane[h][:], in_=hid[h][:])
            for n in range(2):
                nc.tensor.matmul_mx(
                    out=p_banks[h][n][:],
                    lhsT=wb_codes[:, P * n : P * (n + 1)].bitcast(E5M2),
                    lhsT_scale=wb_plane[:, P * n : P * (n + 1)],
                    rhs=hid_codes[h][:].bitcast(E4M3),
                    rhs_scale=hid_plane[h][:],
                    start=False,
                    stop=True,
                )

        def places(n, h):
            return pages[n][:].indirect(place_list[:, h * H // 16 : (h + 1) * H // 16])

        def place_on_scalar(h, n):
            nc.scalar.copy(results[h][n][:], p_banks[h][n][:])
            nc.scalar.activation(places(n, h), results[h][n][:], COPY)

        def place_on_vector(h, n):
            nc.vector.tensor_copy(results[h][n][:], p_banks[h][n][:])
            nc.vector.tensor_copy(places(n, h), results[h][n][:])

        cap(0)
        cap(1)
        floor(0)
        floor(1)
        quantise(0)
        quantise(1)
        for h in range(2):
            place_on_scalar(h, 0)
            place_on_vector(h, 1)
        nc.scalar.dma_start(out=out[0:P, :], in_=pages[0][:])
        nc.sync.dma_start(out=out[P : 2 * P, :], in_=pages[1][:])
